import numpy as np
import ml_dtypes


def mxq(x, axis, fmt="e4m3"):
    dtype, down = {"e4m3": (ml_dtypes.float8_e4m3fn, 7), "e5m2": (ml_dtypes.float8_e5m2, 14)}[fmt]
    v = np.moveaxis(np.asarray(x, np.float32).astype(ml_dtypes.bfloat16).astype(np.float64), axis, -1)
    blocks = v.reshape(v.shape[:-1] + (-1, 32))
    amax = np.abs(blocks).max(-1, keepdims=True)
    byte = np.maximum(np.where(amax > 0, np.frexp(amax)[1] - 1 + 127, 0) - down, 1)
    scale = np.exp2(byte - 127.0)
    codes = (blocks / scale).astype(np.float32).astype(dtype).astype(np.float64)
    return np.moveaxis((codes * scale).reshape(v.shape), -1, axis)


WIDE = False


def mx_kscale(k):
    if not WIDE:
        return np.ones(k)
    levels = np.array([10, -10, 5, -5, 0])
    if k % 512:
        return np.exp2(np.random.permutation(np.resize(levels, k // 32))).repeat(32)
    a = np.empty((k // 512, 16))
    for p in range(k // 512):
        a[p, :8] = np.random.permutation(np.resize(levels, 8))
        for g in range(8):
            far = levels[np.abs(levels - a[p, g]) >= 10]
            a[p, g + 8] = far[np.random.randint(len(far))]
    return np.exp2(a.ravel()).repeat(32)


def f64(x):
    return np.asarray(x).astype(np.float64)


def striped(idx):
    return np.tile(idx.reshape(-1, 16).T, (8, 1)).astype(np.uint16)


def unstriped(offs):
    return offs[:16].T.reshape(-1).astype(np.int64)


def pack_weight(w):
    k, n = w.shape
    w = f64(np.asarray(w, np.float32).astype(ml_dtypes.bfloat16)).reshape(k // 32, 32, n)
    amax = np.abs(w).max(1)
    byte = np.clip(np.where(amax > 0, np.frexp(amax)[1] - 1 + 127 - 7, 1), 1, 254)
    scaled = (w * np.exp2(127.0 - byte)[:, None, :]).reshape(k, n).astype(np.float32)
    words = np.ascontiguousarray(scaled.reshape(k // 512, 128, 4, n).transpose(0, 1, 3, 2)).astype(ml_dtypes.float8_e4m3fn).view(np.uint8)
    return words, np.ascontiguousarray(byte.astype(np.uint8).reshape(k // 512, 16, n))


def unpack_weight(words, scales):
    g, p, n, _ = words.shape
    vals = np.ascontiguousarray(words).view(ml_dtypes.float8_e4m3fn).astype(np.float64) * np.repeat(np.exp2(scales.astype(np.float64) - 127.0), 8, axis=1)[..., None]
    return vals.transpose(0, 1, 3, 2).reshape(g * 512, n)


def relu(v):
    return np.maximum(v, 0.0)


K, T, E, C, N = 1024, 512, 4, 128, 128


def by_expert(wq, xq):
    return np.concatenate([wq[e].T @ xq[:, e * C:(e + 1) * C] for e in range(E)], axis=1)


def setup_inputs():
    n = np.random.standard_normal
    s = mx_kscale(K)[:, None]
    packed = [pack_weight(m) for m in n((E, K, N)) / np.sqrt(K) / s[None]]
    return {
        "xT": (n((K, T)) * s).astype(np.float32),
        "w_words": np.stack([m[0] for m in packed]),
        "w_scales": np.stack([m[1] for m in packed]),
        "b": (0.3 * n((N, E))).astype(np.float32),
        "gate": np.tile(np.random.uniform(0.2, 1.0, E * C), (N, 1)).astype(np.float32),
        "offs": striped(np.random.permutation(T)[:E * C]),
        "dst": striped(np.random.permutation(T)[:E * C]),
    }


def reference(xT, w_words, w_scales, b, gate, offs, dst):
    idx = unstriped(offs)
    w = np.stack([unpack_weight(w_words[e], w_scales[e]) for e in range(E)])
    xq = mxq(f64(xT)[:, idx], 0, "e4m3")
    y = by_expert(w, xq)
    y = relu(y + np.repeat(f64(b), C, axis=1))
    out = np.zeros((N, T))
    out[:, unstriped(dst)] = f64(gate) * y
    return out

@@ -1,0 +1,112 @@
+import concourse.mybir as mybir
+
+F32 = mybir.dt.float32
+BF16 = mybir.dt.bfloat16
+I32 = mybir.dt.int32
+U32 = mybir.dt.uint32
+U16 = mybir.dt.uint16
+U8 = mybir.dt.uint8
+FP8X4 = mybir.dt.float8_e4m3fn_x4
+RELU = mybir.ActivationFunctionType.Relu
+MULT = mybir.AluOpType.mult
+
+P = 128
+PACK = 4
+K = 1024
+T = 512
+E = 4
+C = 128
+N = 128
+PASSES = 2
+FLOPS = 2 * K * N * T
+
+CHUNKS = ((0, 0, 256, 256), (0, 256, 512, 256), (1, 0, 256, 256), (1, 256, 384, 96), (1, 384, 512, 48))
+PLANE = (4, 0)
+
+
+def tile_moe_two_lin_relu_kernel(tc, xT, w_words, w_scales, b, gate, offs, dst, out):
+    nc = tc.nc
+    with tc.tile_pool(name="keep", bufs=1) as keep, tc.psum_pool(name="psum", bufs=1) as psum:
+        offsets = keep.tile([P, T // 16], U16, name="offsets")
+        places = keep.tile([P, T // 16], U16, name="places")
+        warm = keep.tile([P, 1], F32, name="warm")
+        weight_scales = keep.tile([P, E * PASSES, N], U8, name="weight_scales", align_bytes=64)
+        token_scales = keep.tile([P, T], U8, name="token_scales", align_bytes=64)
+        nc.vector.memset(warm[:], 0.0)
+        nc.vector.memset(weight_scales[:].rearrange("p g n -> p (g n)").bitcast(I32), 0)
+        nc.gpsimd.memset(token_scales[:], 0)
+        nc.scalar.activation(warm[:], warm[:], RELU)
+
+        rows = xT.rearrange("(a p j) t -> a p j t", a=PASSES, j=PACK)
+        raws = []
+        for i, (a, t0, t1, _) in enumerate(CHUNKS):
+            raw = keep.tile([P, PACK, t1 - t0], F32, name=f"raw{i}")
+            nc.sync.dma_start(raw[:], rows[a][:, :, t0:t1])
+            raws.append(raw)
+            if i == 0:
+                nc.sync.dma_start(offsets[:], offs)
+        scales_in = w_scales.rearrange("e a q n -> q (e a) n").bitcast(I32)
+        for q in range(4):
+            nc.scalar.dma_start(
+                weight_scales[32 * q : 32 * q + 4, :, :].bitcast(I32),
+                scales_in[4 * q : 4 * q + 4, :, :],
+            )
+        weights = keep.tile([P, E * PASSES, N], U32, name="weights", align_bytes=64)
+        nc.sync.dma_start(weights[:].bitcast(I32), w_words.rearrange("e a p n r -> p (e a) (n r)").bitcast(I32))
+        bias = keep.tile([P, E], F32, name="bias")
+        gates = keep.tile([P, E * C], F32, name="gates")
+        nc.sync.dma_start(gates[:], gate)
+        nc.sync.dma_start(places[:], dst)
+        nc.sync.dma_start(bias[:], b)
+
+        words = [keep.tile([P, T], U32, name=f"words{a}", align_bytes=64) for a in range(PASSES)]
+        slot_words = [keep.tile([P, E * C], U32, name=f"slot_words{a}", align_bytes=64) for a in range(PASSES)]
+        slot_scales = keep.tile([P, E * C], U8, name="slot_scales", align_bytes=64)
+        banks = [psum.tile([N, C], F32, name=f"bank{e}") for e in range(E)]
+        results = [keep.tile([N, C], F32, name=f"result{e}") for e in range(E)]
+        placed = keep.tile([N, T], F32, name="placed")
+
+        def gather_words(a, j0, j1):
+            nc.vector.tensor_copy(slot_words[a][:, j0:j1], words[a][:].indirect(offsets[:, j0 // 16 : j1 // 16]))
+
+        def multiply(e, a):
+            cols = slice(e * C, (e + 1) * C)
+            nc.tensor.matmul_mx(
+                out=banks[e][:],
+                lhsT=weights[:, e * PASSES + a, :].bitcast(FP8X4),
+                lhsT_scale=weight_scales[:, e * PASSES + a, :],
+                rhs=slot_words[a][:, cols].bitcast(FP8X4),
+                rhs_scale=slot_scales[PLANE[a] :, cols],
+                start=(a == 0),
+                stop=(a == PASSES - 1),
+            )
+
+        for i, (a, t0, t1, split) in enumerate(CHUNKS):
+            raw = raws[i]
+            grouped = keep.tile([P, t1 - t0, PACK], BF16, name=f"grouped{i}", align_bytes=64)
+            turned = raw[:].rearrange("p j t -> p t j")
+            if split > 0:
+                nc.scalar.copy(grouped[:, 0:split, :], turned[:, 0:split, :])
+            if split < t1 - t0:
+                nc.vector.tensor_copy(grouped[:, split:, :], turned[:, split:, :])
+            nc.vector.quantize_mx(
+                out=words[a][:, t0:t1].bitcast(FP8X4),
+                scales=token_scales[PLANE[a] :, t0:t1],
+                in_=grouped[:].rearrange("p t j -> p (t j)"),
+            )
+            if a == 0 and t1 == T:
+                gather_words(0, 0, 256)
+                gather_words(0, 256, 512)
+        for e in range(E):
+            j0, j1 = e * C, (e + 1) * C
+            gather_words(1, j0, j1)
+            nc.vector.tensor_copy(slot_scales[:, j0:j1], token_scales[:].indirect(offsets[:, j0 // 16 : j1 // 16]))
+            for a in range(PASSES):
+                multiply(e, a)
+            nc.scalar.activation(results[e][:], banks[e][:], RELU, bias=bias[:, e : e + 1])
+        for e in range(E):
+            j0, j1 = e * C, (e + 1) * C
+            weighted = keep.tile([N, C], F32, name=f"weighted{e}")
+            nc.gpsimd.tensor_tensor(weighted[:], results[e][:], gates[:, j0:j1], MULT)
+            nc.vector.tensor_copy(placed[:].indirect(places[:, j0 // 16 : j1 // 16]), weighted[:])
+        nc.sync.dma_start(out, placed[:])

@@ -20,7 +20,7 @@ N = 128
 PASSES = 2
 FLOPS = 2 * K * N * T
 
-CHUNKS = ((0, 0, 256, 256), (0, 256, 512, 256), (1, 0, 256, 256), (1, 256, 384, 96), (1, 384, 512, 48))
+CHUNKS = ((0, 0, 256, 104), (0, 256, 512, 104), (1, 0, 256, 216), (1, 256, 512, 112))
 PLANE = (4, 0)
 
 
@@ -47,12 +47,14 @@ def tile_moe_two_lin_relu_kernel(tc, xT, w_words, w_scales, b, gate, offs, dst, 
                 nc.sync.dma_start(offsets[:], offs)
         scales_in = w_scales.rearrange("e a q n -> q (e a) n").bitcast(I32)
         for q in range(4):
-            nc.scalar.dma_start(
+            nc.sync.dma_start(
                 weight_scales[32 * q : 32 * q + 4, :, :].bitcast(I32),
                 scales_in[4 * q : 4 * q + 4, :, :],
             )
         weights = keep.tile([P, E * PASSES, N], U32, name="weights", align_bytes=64)
-        nc.sync.dma_start(weights[:].bitcast(I32), w_words.rearrange("e a p n r -> p (e a) (n r)").bitcast(I32))
+        words_in = w_words.rearrange("e a p n r -> p (e a) (n r)").bitcast(I32)
+        for g0 in range(0, E * PASSES, 4):
+            nc.sync.dma_start(weights[:, g0 : g0 + 4, :].bitcast(I32), words_in[:, g0 : g0 + 4, :])
         bias = keep.tile([P, E], F32, name="bias")
         gates = keep.tile([P, E * C], F32, name="gates")
         nc.sync.dma_start(gates[:], gate)

@@ -108,7 +108,5 @@ def tile_moe_two_lin_relu_kernel(tc, xT, w_words, w_scales, b, gate, offs, dst, 
             nc.scalar.activation(results[e][:], banks[e][:], RELU, bias=bias[:, e : e + 1])
         for e in range(E):
             j0, j1 = e * C, (e + 1) * C
-            weighted = keep.tile([N, C], F32, name=f"weighted{e}")
-            nc.gpsimd.tensor_tensor(weighted[:], results[e][:], gates[:, j0:j1], MULT)
-            nc.vector.tensor_copy(placed[:].indirect(places[:, j0 // 16 : j1 // 16]), weighted[:])
+            nc.vector.tensor_tensor(placed[:].indirect(places[:, j0 // 16 : j1 // 16]), results[e][:], gates[:, j0:j1], MULT)
         nc.sync.dma_start(out, placed[:])

@@ -20,7 +20,7 @@ N = 128
 PASSES = 2
 FLOPS = 2 * K * N * T
 
-CHUNKS = ((0, 0, 256, 104), (0, 256, 512, 104), (1, 0, 256, 216), (1, 256, 512, 112))
+CHUNKS = ((0, 0, 256, 168), (0, 256, 512, 168), (1, 0, 256, 0), (1, 256, 512, 112))
 PLANE = (4, 0)
 
 
@@ -38,34 +38,33 @@ def tile_moe_two_lin_relu_kernel(tc, xT, w_words, w_scales, b, gate, offs, dst, 
         nc.scalar.activation(warm[:], warm[:], RELU)
 
         rows = xT.rearrange("(a p j) t -> a p j t", a=PASSES, j=PACK)
-        raws = []
-        for i, (a, t0, t1, _) in enumerate(CHUNKS):
-            raw = keep.tile([P, PACK, t1 - t0], F32, name=f"raw{i}")
-            nc.sync.dma_start(raw[:], rows[a][:, :, t0:t1])
-            raws.append(raw)
-            if i == 0:
-                nc.sync.dma_start(offsets[:], offs)
+        raw_first = keep.tile([P, PACK, T], F32, name="raw_first")
+        nc.sync.dma_start(raw_first[:], rows[0])
+        nc.sync.dma_start(offsets[:], offs)
+        raws = [raw_first[:, :, 0:256], raw_first[:, :, 256:512]]
+        for h in range(2):
+            raw = keep.tile([P, PACK, 256], F32, name=f"raw{h}")
+            nc.sync.dma_start(raw[:], rows[1][:, :, h * 256 : (h + 1) * 256])
+            raws.append(raw[:])
+        bias = keep.tile([P, E], F32, name="bias")
+        weights = keep.tile([P, E * PASSES, N], U32, name="weights", align_bytes=64)
+        gates = keep.tile([P, E * C], F32, name="gates")
         scales_in = w_scales.rearrange("e a q n -> q (e a) n").bitcast(I32)
         for q in range(4):
             nc.sync.dma_start(
                 weight_scales[32 * q : 32 * q + 4, :, :].bitcast(I32),
                 scales_in[4 * q : 4 * q + 4, :, :],
             )
-        weights = keep.tile([P, E * PASSES, N], U32, name="weights", align_bytes=64)
-        words_in = w_words.rearrange("e a p n r -> p (e a) (n r)").bitcast(I32)
-        for g0 in range(0, E * PASSES, 4):
-            nc.sync.dma_start(weights[:, g0 : g0 + 4, :].bitcast(I32), words_in[:, g0 : g0 + 4, :])
-        bias = keep.tile([P, E], F32, name="bias")
-        gates = keep.tile([P, E * C], F32, name="gates")
-        nc.sync.dma_start(gates[:], gate)
-        nc.sync.dma_start(places[:], dst)
         nc.sync.dma_start(bias[:], b)
+        nc.sync.dma_start(places[:], dst)
+        nc.sync.dma_start(weights[:].bitcast(I32), w_words.rearrange("e a p n r -> p (e a) (n r)").bitcast(I32))
+        nc.sync.dma_start(gates[:], gate)
 
         words = [keep.tile([P, T], U32, name=f"words{a}", align_bytes=64) for a in range(PASSES)]
         slot_words = [keep.tile([P, E * C], U32, name=f"slot_words{a}", align_bytes=64) for a in range(PASSES)]
         slot_scales = keep.tile([P, E * C], U8, name="slot_scales", align_bytes=64)
         banks = [psum.tile([N, C], F32, name=f"bank{e}") for e in range(E)]
-        results = [keep.tile([N, C], F32, name=f"result{e}") for e in range(E)]
+        results = [keep.tile([N, 2 * C], F32, name=f"result{h}") for h in range(2)]
         placed = keep.tile([N, T], F32, name="placed")
 
         def gather_words(a, j0, j1):
@@ -83,30 +82,48 @@ def tile_moe_two_lin_relu_kernel(tc, xT, w_words, w_scales, b, gate, offs, dst, 
                 stop=(a == PASSES - 1),
             )
 
-        for i, (a, t0, t1, split) in enumerate(CHUNKS):
-            raw = raws[i]
-            grouped = keep.tile([P, t1 - t0, PACK], BF16, name=f"grouped{i}", align_bytes=64)
-            turned = raw[:].rearrange("p j t -> p t j")
-            if split > 0:
-                nc.scalar.copy(grouped[:, 0:split, :], turned[:, 0:split, :])
-            if split < t1 - t0:
-                nc.vector.tensor_copy(grouped[:, split:, :], turned[:, split:, :])
+        grouped = [
+            keep.tile([P, t1 - t0, PACK], BF16, name=f"grouped{i}", align_bytes=64)
+            for i, (_, t0, t1, _) in enumerate(CHUNKS)
+        ]
+
+        def interleave(i):
+            _, t0, t1, split = CHUNKS[i]
+            for copy, c0, c1 in ((nc.vector.tensor_copy, 0, split), (nc.scalar.copy, split, t1 - t0)):
+                if c0 < c1:
+                    copy(
+                        grouped[i][:, c0:c1, :].rearrange("p (c i) j -> p c j i", i=4),
+                        raws[i][:, :, c0:c1].rearrange("p j (c i) -> p c j i", i=4),
+                    )
+
+        def quantise(i, c0, c1):
+            a, t0, _, _ = CHUNKS[i]
             nc.vector.quantize_mx(
-                out=words[a][:, t0:t1].bitcast(FP8X4),
-                scales=token_scales[PLANE[a] :, t0:t1],
-                in_=grouped[:].rearrange("p t j -> p (t j)"),
+                out=words[a][:, t0 + c0 : t0 + c1].bitcast(FP8X4),
+                scales=token_scales[PLANE[a] :, t0 + c0 : t0 + c1],
+                in_=grouped[i][:, c0:c1, :].rearrange("p t j -> p (t j)"),
             )
-            if a == 0 and t1 == T:
-                gather_words(0, 0, 256)
-                gather_words(0, 256, 512)
-        for e in range(E):
-            j0, j1 = e * C, (e + 1) * C
-            gather_words(1, j0, j1)
+
+        interleave(0)
+        interleave(1)
+        quantise(0, 0, 256)
+        quantise(1, 0, 256)
+        gather_words(0, 0, 256)
+        gather_words(0, 256, 512)
+        interleave(2)
+        interleave(3)
+        quantise(2, 0, 256)
+        quantise(3, 0, 256)
+        for h in range(2):
+            j0, j1 = 2 * h * C, 2 * (h + 1) * C
             nc.vector.tensor_copy(slot_scales[:, j0:j1], token_scales[:].indirect(offsets[:, j0 // 16 : j1 // 16]))
-            for a in range(PASSES):
-                multiply(e, a)
-            nc.scalar.activation(results[e][:], banks[e][:], RELU, bias=bias[:, e : e + 1])
-        for e in range(E):
-            j0, j1 = e * C, (e + 1) * C
-            nc.vector.tensor_tensor(placed[:].indirect(places[:, j0 // 16 : j1 // 16]), results[e][:], gates[:, j0:j1], MULT)
+            gather_words(1, j0, j1)
+            for e in (2 * h, 2 * h + 1):
+                multiply(e, 0)
+            for e in (2 * h, 2 * h + 1):
+                multiply(e, 1)
+                nc.scalar.activation(results[h][:, (e % 2) * C : (e % 2 + 1) * C], banks[e][:], RELU, bias=bias[:, e : e + 1])
+        for h in range(2):
+            j0, j1 = 2 * h * C, 2 * (h + 1) * C
+            nc.vector.tensor_tensor(placed[:].indirect(places[:, j0 // 16 : j1 // 16]), results[h][:], gates[:, j0:j1], MULT)
         nc.sync.dma_start(out, placed[:])

import concourse.mybir as mybir

F32 = mybir.dt.float32
BF16 = mybir.dt.bfloat16
I32 = mybir.dt.int32
U32 = mybir.dt.uint32
U16 = mybir.dt.uint16
U8 = mybir.dt.uint8
FP8X4 = mybir.dt.float8_e4m3fn_x4
RELU = mybir.ActivationFunctionType.Relu
MULT = mybir.AluOpType.mult

P = 128
PACK = 4
K = 1024
T = 512
E = 4
C = 128
N = 128
PASSES = 2
FLOPS = 2 * K * N * T

CHUNKS = ((0, 0, 256, 168), (0, 256, 512, 168), (1, 0, 256, 0), (1, 256, 512, 112))
PLANE = (4, 0)


def tile_moe_two_lin_relu_kernel(tc, xT, w_words, w_scales, b, gate, offs, dst, out):
    nc = tc.nc
    with tc.tile_pool(name="keep", bufs=1) as keep, tc.psum_pool(name="psum", bufs=1) as psum:
        offsets = keep.tile([P, T // 16], U16, name="offsets")
        places = keep.tile([P, T // 16], U16, name="places")
        warm = keep.tile([P, 1], F32, name="warm")
        weight_scales = keep.tile([P, E * PASSES, N], U8, name="weight_scales", align_bytes=64)
        token_scales = keep.tile([P, T], U8, name="token_scales", align_bytes=64)
        nc.vector.memset(warm[:], 0.0)
        nc.vector.memset(weight_scales[:].rearrange("p g n -> p (g n)").bitcast(I32), 0)
        nc.gpsimd.memset(token_scales[:], 0)
        nc.scalar.activation(warm[:], warm[:], RELU)

        rows = xT.rearrange("(a p j) t -> a p j t", a=PASSES, j=PACK)
        raw_first = keep.tile([P, PACK, T], F32, name="raw_first")
        nc.sync.dma_start(raw_first[:], rows[0])
        nc.sync.dma_start(offsets[:], offs)
        raws = [raw_first[:, :, 0:256], raw_first[:, :, 256:512]]
        for h in range(2):
            raw = keep.tile([P, PACK, 256], F32, name=f"raw{h}")
            nc.sync.dma_start(raw[:], rows[1][:, :, h * 256 : (h + 1) * 256])
            raws.append(raw[:])
        bias = keep.tile([P, E], F32, name="bias")
        weights = keep.tile([P, E * PASSES, N], U32, name="weights", align_bytes=64)
        gates = keep.tile([P, E * C], F32, name="gates")
        scales_in = w_scales.rearrange("e a q n -> q (e a) n").bitcast(I32)
        for q in range(4):
            nc.sync.dma_start(
                weight_scales[32 * q : 32 * q + 4, :, :].bitcast(I32),
                scales_in[4 * q : 4 * q + 4, :, :],
            )
        nc.sync.dma_start(bias[:], b)
        nc.sync.dma_start(places[:], dst)
        nc.sync.dma_start(weights[:].bitcast(I32), w_words.rearrange("e a p n r -> p (e a) (n r)").bitcast(I32))
        nc.sync.dma_start(gates[:], gate)

        words = [keep.tile([P, T], U32, name=f"words{a}", align_bytes=64) for a in range(PASSES)]
        slot_words = [keep.tile([P, E * C], U32, name=f"slot_words{a}", align_bytes=64) for a in range(PASSES)]
        slot_scales = keep.tile([P, E * C], U8, name="slot_scales", align_bytes=64)
        banks = [psum.tile([N, C], F32, name=f"bank{e}") for e in range(E)]
        results = [keep.tile([N, 2 * C], F32, name=f"result{h}") for h in range(2)]
        placed = keep.tile([N, T], F32, name="placed")

        def gather_words(a, j0, j1):
            nc.vector.tensor_copy(slot_words[a][:, j0:j1], words[a][:].indirect(offsets[:, j0 // 16 : j1 // 16]))

        def multiply(e, a):
            cols = slice(e * C, (e + 1) * C)
            nc.tensor.matmul_mx(
                out=banks[e][:],
                lhsT=weights[:, e * PASSES + a, :].bitcast(FP8X4),
                lhsT_scale=weight_scales[:, e * PASSES + a, :],
                rhs=slot_words[a][:, cols].bitcast(FP8X4),
                rhs_scale=slot_scales[PLANE[a] :, cols],
                start=(a == 0),
                stop=(a == PASSES - 1),
            )

        grouped = [
            keep.tile([P, t1 - t0, PACK], BF16, name=f"grouped{i}", align_bytes=64)
            for i, (_, t0, t1, _) in enumerate(CHUNKS)
        ]

        def interleave(i):
            _, t0, t1, split = CHUNKS[i]
            for copy, c0, c1 in ((nc.vector.tensor_copy, 0, split), (nc.scalar.copy, split, t1 - t0)):
                if c0 < c1:
                    copy(
                        grouped[i][:, c0:c1, :].rearrange("p (c i) j -> p c j i", i=4),
                        raws[i][:, :, c0:c1].rearrange("p j (c i) -> p c j i", i=4),
                    )

        def quantise(i, c0, c1):
            a, t0, _, _ = CHUNKS[i]
            nc.vector.quantize_mx(
                out=words[a][:, t0 + c0 : t0 + c1].bitcast(FP8X4),
                scales=token_scales[PLANE[a] :, t0 + c0 : t0 + c1],
                in_=grouped[i][:, c0:c1, :].rearrange("p t j -> p (t j)"),
            )

        interleave(0)
        interleave(1)
        quantise(0, 0, 256)
        quantise(1, 0, 256)
        gather_words(0, 0, 256)
        gather_words(0, 256, 512)
        interleave(2)
        interleave(3)
        quantise(2, 0, 256)
        quantise(3, 0, 256)
        for h in range(2):
            j0, j1 = 2 * h * C, 2 * (h + 1) * C
            nc.vector.tensor_copy(slot_scales[:, j0:j1], token_scales[:].indirect(offsets[:, j0 // 16 : j1 // 16]))
            gather_words(1, j0, j1)
            for e in (2 * h, 2 * h + 1):
                multiply(e, 0)
            for e in (2 * h, 2 * h + 1):
                multiply(e, 1)
                nc.scalar.activation(results[h][:, (e % 2) * C : (e % 2 + 1) * C], banks[e][:], RELU, bias=bias[:, e : e + 1])
        for h in range(2):
            j0, j1 = 2 * h * C, 2 * (h + 1) * C
            nc.vector.tensor_tensor(placed[:].indirect(places[:, j0 // 16 : j1 // 16]), results[h][:], gates[:, j0:j1], MULT)
        nc.sync.dma_start(out, placed[:])
